import numpy as np
import ml_dtypes


def mxq(x, axis, fmt="e4m3"):
    dtype, down = {"e4m3": (ml_dtypes.float8_e4m3fn, 7), "e5m2": (ml_dtypes.float8_e5m2, 14)}[fmt]
    v = np.moveaxis(np.asarray(x, np.float32).astype(ml_dtypes.bfloat16).astype(np.float64), axis, -1)
    blocks = v.reshape(v.shape[:-1] + (-1, 32))
    amax = np.abs(blocks).max(-1, keepdims=True)
    byte = np.maximum(np.where(amax > 0, np.frexp(amax)[1] - 1 + 127, 0) - down, 1)
    scale = np.exp2(byte - 127.0)
    codes = (blocks / scale).astype(np.float32).astype(dtype).astype(np.float64)
    return np.moveaxis((codes * scale).reshape(v.shape), -1, axis)


WIDE = False


def mx_kscale(k):
    if not WIDE:
        return np.ones(k)
    levels = np.array([10, -10, 5, -5, 0])
    if k % 512:
        return np.exp2(np.random.permutation(np.resize(levels, k // 32))).repeat(32)
    a = np.empty((k // 512, 16))
    for p in range(k // 512):
        a[p, :8] = np.random.permutation(np.resize(levels, 8))
        for g in range(8):
            far = levels[np.abs(levels - a[p, g]) >= 10]
            a[p, g + 8] = far[np.random.randint(len(far))]
    return np.exp2(a.ravel()).repeat(32)


def f64(x):
    return np.asarray(x).astype(np.float64)


def striped(idx):
    return np.tile(idx.reshape(-1, 16).T, (8, 1)).astype(np.uint16)


def unstriped(offs):
    return offs[:16].T.reshape(-1).astype(np.int64)


def striped8(idx):
    return np.concatenate([x.reshape(-1, 16).T for x in idx]).astype(np.uint16)


def runs(offs, k):
    lists = np.stack([offs[16 * r : 16 * r + 16].T.reshape(-1) for r in range(8)]).astype(np.int64)
    return lists[np.arange(k) % 512 // 64]


def pack_weight(w):
    k, n = w.shape
    w = f64(np.asarray(w, np.float32).astype(ml_dtypes.bfloat16)).reshape(k // 32, 32, n)
    amax = np.abs(w).max(1)
    byte = np.clip(np.where(amax > 0, np.frexp(amax)[1] - 1 + 127 - 7, 1), 1, 254)
    scaled = (w * np.exp2(127.0 - byte)[:, None, :]).reshape(k, n).astype(np.float32)
    words = np.ascontiguousarray(scaled.reshape(k // 512, 128, 4, n).transpose(0, 1, 3, 2)).astype(ml_dtypes.float8_e4m3fn).view(np.uint8)
    return words, np.ascontiguousarray(byte.astype(np.uint8).reshape(k // 512, 16, n))


def unpack_weight(words, scales):
    g, p, n, _ = words.shape
    vals = np.ascontiguousarray(words).view(ml_dtypes.float8_e4m3fn).astype(np.float64) * np.repeat(np.exp2(scales.astype(np.float64) - 127.0), 8, axis=1)[..., None]
    return vals.transpose(0, 1, 3, 2).reshape(g * 512, n)


K, T, S, N, H, W = 512, 2048, 512, 512, 512, 256


def setup_inputs():
    n = np.random.standard_normal
    s = mx_kscale(K)[:, None]
    u = mx_kscale(H)
    packed_xT = pack_weight(n((K, T)) * s)
    perm = np.stack([np.random.permutation(S) for _ in range(8)])
    return {
        "x_words": packed_xT[0],
        "x_scales": packed_xT[1],
        "w1": (n((K, H)) / np.sqrt(K) / s * u).astype(np.float32),
        "w2": (n((H, H)) / np.sqrt(H) / u[:, None] * u).astype(np.float32),
        "w3": (n((H, N)) / np.sqrt(H) / u[:, None]).astype(np.float32),
        "res": n((N, S)).astype(np.float32),
        "offs": striped(np.random.permutation(T)[:S]),
        "n1": striped8(perm[:, :W]),
        "n2": striped8(perm[:, W:]),
        "n3": striped8(np.stack([np.random.permutation(S) for _ in range(8)])),
        "n4": striped8(np.stack([np.random.permutation(S) for _ in range(8)])),
    }


def reference(x_words, x_scales, w1, w2, w3, res, offs, n1, n2, n3, n4):
    xq = unpack_weight(x_words, x_scales)[:, unstriped(offs)]
    y = mxq(f64(w1), 0, "e4m3").T @ xq
    pa = y[np.arange(H)[:, None], runs(n1, H)]
    pb = y[np.arange(H)[:, None], runs(n2, H)]
    ra = np.maximum(pa, pb)
    z = y.copy()
    z[np.arange(H)[:, None], runs(n1, H)] = ra
    h = mxq(f64(w2), 0, "e4m3").T @ mxq(z, 0, "e4m3")
    pa2 = h[np.arange(H)[:, None], runs(n3, H)]
    pb2 = h[np.arange(H)[:, None], runs(n4, H)]
    z2 = np.maximum(np.maximum(h, pa2), pb2) - (0.5 * (np.minimum(np.minimum(h, pa2), pb2)))
    return f64(res) + (mxq(f64(w3), 0, "e4m3").T @ mxq(z2, 0, "e4m3"))

@@ -1,0 +1,194 @@
+from contextlib import ExitStack
+
+import concourse.mybir as mybir
+
+K, T, S, W = 512, 2048, 512, 256
+P, PACK = 128, 4
+FLOPS = 3 * 2 * K * K * S
+
+F32, BF16 = mybir.dt.float32, mybir.dt.bfloat16
+I32, U32, U16, U8 = mybir.dt.int32, mybir.dt.uint32, mybir.dt.uint16, mybir.dt.uint8
+FP8X4 = mybir.dt.float8_e4m3fn_x4
+ALU = mybir.AluOpType
+ACT = mybir.ActivationFunctionType
+
+BLOCKS = [(0, 256), (256, 128), (384, 128)]
+Z_SPLIT = 336
+
+
+def tile_picked_deepfillrange_none_p_kernel(
+    tc, x_words, x_scales, w1, w2, w3, res, offs, n1, n2, n3, n4, out
+):
+    nc = tc.nc
+    with ExitStack() as ctx:
+        keep = ctx.enter_context(tc.tile_pool(name="keep", bufs=1))
+        work = ctx.enter_context(tc.tile_pool(name="work", bufs=2))
+        psum = ctx.enter_context(tc.psum_pool(name="psum", bufs=1))
+
+        def load_list(src, name):
+            tile = keep.tile(list(src.shape), U16, name=name)
+            nc.sync.dma_start(tile[:], src)
+            return tile
+
+        def load_rows(src, name):
+            tile = keep.tile([P, PACK, src.shape[1]], F32, name=name)
+            nc.sync.dma_start(tile[:], src.rearrange("(p j) c -> p j c", j=PACK))
+            return tile
+
+        def mx_tiles(name):
+            codes = keep.tile([P, S], U32, name=name + "_codes", align_bytes=64)
+            scales = keep.tile([P, S], U8, name=name + "_scales", align_bytes=64)
+            return codes, scales
+
+        def quantize(operand, grouped, cols):
+            codes, scales = operand
+            nc.vector.quantize_mx(
+                out=codes[:, cols].bitcast(FP8X4),
+                scales=scales[:, cols],
+                in_=grouped[:, PACK * cols.start : PACK * cols.stop],
+            )
+
+        def product(acc, weights, tile_no, moving, cols):
+            rows = slice(tile_no * P, (tile_no + 1) * P)
+            nc.tensor.matmul_mx(
+                out=acc,
+                lhsT=weights[0][:, rows].bitcast(FP8X4),
+                lhsT_scale=weights[1][:, rows],
+                rhs=moving[0][:, cols].bitcast(FP8X4),
+                rhs_scale=moving[1][:, cols],
+                start=True,
+                stop=True,
+            )
+
+        def deal(copy, grouped, raw, m0):
+            count = raw.shape[2] // PACK
+            dst = grouped[:].rearrange("p (t m j) -> p m j t", t=PACK, j=PACK)[:, m0 : m0 + count]
+            copy(dst, raw[:].rearrange("p j (m t) -> p m j t", t=PACK))
+
+        def weave(copy, grouped, planes):
+            copy(
+                grouped.rearrange("p (c i j) -> p c j i", i=4, j=PACK),
+                planes.rearrange("p j (c i) -> p c j i", i=4),
+            )
+
+        offs_t = load_list(offs, "offs_t")
+        table_scales = keep.tile([P, T], U8, name="table_scales")
+        nc.vector.memset(table_scales[:].bitcast(I32), 0)
+        for q in range(4):
+            nc.sync.dma_start(
+                table_scales[32 * q : 32 * q + 4, :].bitcast(I32),
+                x_scales[0, 4 * q : 4 * q + 4, :].bitcast(I32),
+            )
+        table_words = keep.tile([P, T], I32, name="table_words")
+        nc.sync.dma_start(table_words[:], x_words[0].rearrange("p n r -> p (n r)").bitcast(I32))
+        w1_raw = [load_rows(w1[:, h * 256 : (h + 1) * 256], "w1_raw%d" % h) for h in range(2)]
+        n1_t = load_list(n1, "n1_t")
+        n2_t = load_list(n2, "n2_t")
+        w2_raw = load_rows(w2, "w2_raw")
+        n3_t = load_list(n3, "n3_t")
+        n4_t = load_list(n4, "n4_t")
+        w3_raw = load_rows(w3, "w3_raw")
+        res_t = keep.tile([P, PACK, S], F32, name="res_t")
+        nc.sync.dma_start(res_t[:], res.rearrange("(b p) j -> p b j", p=P))
+
+        x_op = mx_tiles("x")
+        nc.vector.tensor_copy(x_op[1][:], table_scales[:].indirect(offs_t[:]))
+        nc.vector.tensor_copy(x_op[0][:], table_words[:].bitcast(U32).indirect(offs_t[:]))
+
+        w1_bf = keep.tile([P, PACK * K], BF16, name="w1_bf", align_bytes=64)
+        deal(nc.scalar.copy, w1_bf, w1_raw[0], 0)
+        deal(nc.vector.tensor_copy, w1_bf, w1_raw[1], 64)
+        w1_op = mx_tiles("w1")
+        banks = [psum.tile([P, S], F32, name="y_ps%d" % t, tag="bank%d" % t) for t in range(PACK)]
+        z = [keep.tile([P, S], F32, name="z%d" % t) for t in range(PACK)]
+        for t in range(PACK):
+            quantize(w1_op, w1_bf, slice(t * P, (t + 1) * P))
+            product(banks[t][:], w1_op, t, x_op, slice(0, S))
+            nc.scalar.copy(z[t][:], banks[t][:])
+
+        w2_bf = keep.tile([P, PACK * K], BF16, name="w2_bf", align_bytes=64)
+        w2_op = mx_tiles("w2")
+        w3_bf = keep.tile([P, PACK * K], BF16, name="w3_bf", align_bytes=64)
+        w3_op = mx_tiles("w3")
+
+        z_planes = keep.tile([P, PACK, S], BF16, name="z_planes")
+        pa = [keep.tile([P, W], F32, name="pa%d" % t) for t in range(PACK)]
+        gain = [keep.tile([P, W], F32, name="gain%d" % t) for t in range(PACK)]
+
+        def fetch_pairs(t):
+            diff = work.tile([P, W], F32, name="diff")
+            nc.vector.tensor_copy(pa[t][:], z[t][:].indirect(n1_t[:]))
+            nc.vector.tensor_tensor(diff[:], z[t][:].indirect(n2_t[:]), pa[t][:], ALU.subtract)
+            nc.scalar.activation(gain[t][:], diff[:], ACT.Relu)
+
+        def put_back(t):
+            nc.vector.tensor_tensor(z[t][:].indirect(n1_t[:]), pa[t][:], gain[t][:], ALU.add)
+            copy = nc.vector.tensor_copy if t == PACK - 1 else nc.scalar.copy
+            copy(z_planes[:, t, :], z[t][:])
+
+        fetch_pairs(0)
+        for t in range(PACK):
+            if t + 1 < PACK:
+                fetch_pairs(t + 1)
+            put_back(t)
+            if t == 0:
+                deal(nc.scalar.copy, w2_bf, w2_raw, 0)
+            if t == 1:
+                quantize(w2_op, w2_bf, slice(0, K))
+                weave(nc.scalar.copy, w3_bf[:], w3_raw[:])
+
+        z_bf = keep.tile([P, PACK * S], BF16, name="z_bf", align_bytes=64)
+        weave(nc.vector.tensor_copy, z_bf[:, : PACK * Z_SPLIT], z_planes[:, :, :Z_SPLIT])
+        weave(nc.scalar.copy, z_bf[:, PACK * Z_SPLIT :], z_planes[:, :, Z_SPLIT:])
+        z_op = mx_tiles("z")
+        halves = [slice(0, S // 2), slice(S // 2, S)]
+        for cols in halves:
+            quantize(z_op, z_bf, cols)
+        quantize(w3_op, w3_bf, slice(0, K))
+
+        banks = [psum.tile([P, S], F32, name="h_ps%d" % t, tag="bank%d" % t) for t in range(PACK)]
+        half_h = [keep.tile([P, S], F32, name="half_h%d" % t) for t in range(PACK)]
+        here = keep.tile([P, PACK, S], F32, name="here")
+        for t in range(PACK):
+            for cols in halves:
+                product(banks[t][:, cols], w2_op, t, z_op, cols)
+            nc.scalar.activation(half_h[t][:], banks[t][:], ACT.Copy, scale=0.5)
+            nc.scalar.activation(here[:, t, :], banks[t][:], ACT.Copy, scale=0.5)
+
+        z2_bf = keep.tile([P, PACK * S], BF16, name="z2_bf", align_bytes=64)
+        z2_op = mx_tiles("z2")
+        out_view = out.rearrange("(b p) j -> p b j", p=P)
+        for j0, width in BLOCKS:
+            cols = slice(j0, j0 + width)
+            entries = slice(j0 // 16, (j0 + width) // 16)
+            z2 = work.tile([P, PACK, width], F32, name="z2")
+            da = work.tile([P, PACK, width], F32, name="da")
+            db = work.tile([P, PACK, width], F32, name="db")
+            up = work.tile([P, PACK, width], F32, name="up")
+            down = work.tile([P, PACK, width], F32, name="down")
+            both = work.tile([P, PACK, width], F32, name="both")
+            pairs = [slice(0, 2), slice(2, 4)]
+            for pair in pairs:
+                for t in range(pair.start, pair.stop):
+                    nc.vector.tensor_tensor(da[:, t, :], half_h[t][:].indirect(n3_t[:, entries]), here[:, t, cols], ALU.subtract)
+                    nc.vector.tensor_tensor(db[:, t, :], half_h[t][:].indirect(n4_t[:, entries]), here[:, t, cols], ALU.subtract)
+            for pair in pairs:
+                nc.vector.scalar_tensor_tensor(up[:, pair], da[:, pair], 0.0, db[:, pair], ALU.max, ALU.max)
+                nc.vector.scalar_tensor_tensor(down[:, pair], da[:, pair], 0.0, db[:, pair], ALU.min, ALU.min)
+            for pair in pairs:
+                nc.vector.scalar_tensor_tensor(both[:, pair], up[:, pair], 2.0, down[:, pair], ALU.mult, ALU.subtract)
+            for pair in pairs:
+                nc.vector.tensor_tensor(z2[:, pair], both[:, pair], here[:, pair, cols], ALU.add)
+            copy = nc.vector.tensor_copy if j0 + width == S else nc.scalar.copy
+            weave(copy, z2_bf[:, PACK * j0 : PACK * (j0 + width)], z2[:])
+            quantize(z2_op, z2_bf, cols)
+            result = work.tile([P, PACK, width], F32, name="result")
+            per_bank = S // width
+            for b0 in range(0, PACK, per_bank):
+                acc = psum.tile([P, per_bank, width], F32, name="acc", tag="acc", bufs=3)
+                for b in range(per_bank):
+                    product(acc[:, b, :], w3_op, b0 + b, z2_op, cols)
+                nc.vector.tensor_tensor(
+                    result[:, b0 : b0 + per_bank, :], acc[:], res_t[:, b0 : b0 + per_bank, cols], ALU.add
+                )
+            nc.sync.dma_start(out_view[:, :, cols], result[:])

@@ -1,6 +1,7 @@
 from contextlib import ExitStack
 
 import concourse.mybir as mybir
+from concourse.masks import make_identity
 
 K, T, S, W = 512, 2048, 512, 256
 P, PACK = 128, 4
@@ -12,8 +13,7 @@ FP8X4 = mybir.dt.float8_e4m3fn_x4
 ALU = mybir.AluOpType
 ACT = mybir.ActivationFunctionType
 
-BLOCKS = [(0, 256), (256, 128), (384, 128)]
-Z_SPLIT = 336
+Z_SPLIT = 320
 
 
 def tile_picked_deepfillrange_none_p_kernel(
@@ -63,7 +63,12 @@ def tile_picked_deepfillrange_none_p_kernel(
         def deal(copy, grouped, raw, m0):
             count = raw.shape[2] // PACK
             dst = grouped[:].rearrange("p (t m j) -> p m j t", t=PACK, j=PACK)[:, m0 : m0 + count]
-            copy(dst, raw[:].rearrange("p j (m t) -> p m j t", t=PACK))
+            copy(dst, raw.rearrange("p j (m t) -> p m j t", t=PACK))
+
+        def deal_pair(copy, grouped, raw, m0, pair):
+            count = raw.shape[2] // PACK
+            dst = grouped[:].rearrange("p (t m j) -> p m j t", t=PACK, j=PACK)[:, m0 : m0 + count, :, pair]
+            copy(dst, raw.rearrange("p j (m t) -> p m j t", t=PACK)[:, :, :, pair])
 
         def weave(copy, grouped, planes):
             copy(
@@ -71,17 +76,18 @@ def tile_picked_deepfillrange_none_p_kernel(
                 planes.rearrange("p j (c i) -> p c j i", i=4),
             )
 
+        landed_scales = keep.tile([P, T // 4], I32, name="landed_scales")
+        quadrants = [slice(32 * q, 32 * q + 4) for q in range(4)]
+        for q, rows in enumerate(quadrants):
+            nc.sync.dma_start(landed_scales[rows, :], x_scales[0, 4 * q : 4 * q + 4, :].bitcast(I32))
         offs_t = load_list(offs, "offs_t")
-        table_scales = keep.tile([P, T], U8, name="table_scales")
-        nc.vector.memset(table_scales[:].bitcast(I32), 0)
-        for q in range(4):
-            nc.sync.dma_start(
-                table_scales[32 * q : 32 * q + 4, :].bitcast(I32),
-                x_scales[0, 4 * q : 4 * q + 4, :].bitcast(I32),
-            )
         table_words = keep.tile([P, T], I32, name="table_words")
         nc.sync.dma_start(table_words[:], x_words[0].rearrange("p n r -> p (n r)").bitcast(I32))
         w1_raw = [load_rows(w1[:, h * 256 : (h + 1) * 256], "w1_raw%d" % h) for h in range(2)]
+        table_scales = keep.tile([P, T], U8, name="table_scales")
+        nc.vector.memset(table_scales[:].bitcast(I32), 0)
+        for rows in quadrants:
+            nc.vector.tensor_copy(table_scales[rows, :].bitcast(I32), landed_scales[rows, :])
         n1_t = load_list(n1, "n1_t")
         n2_t = load_list(n2, "n2_t")
         w2_raw = load_rows(w2, "w2_raw")
@@ -91,104 +97,194 @@ def tile_picked_deepfillrange_none_p_kernel(
         res_t = keep.tile([P, PACK, S], F32, name="res_t")
         nc.sync.dma_start(res_t[:], res.rearrange("(b p) j -> p b j", p=P))
 
+        identity = keep.tile([P, P], F32, name="identity")
+        make_identity(nc, identity[:])
+
         x_op = mx_tiles("x")
         nc.vector.tensor_copy(x_op[1][:], table_scales[:].indirect(offs_t[:]))
         nc.vector.tensor_copy(x_op[0][:], table_words[:].bitcast(U32).indirect(offs_t[:]))
 
         w1_bf = keep.tile([P, PACK * K], BF16, name="w1_bf", align_bytes=64)
-        deal(nc.scalar.copy, w1_bf, w1_raw[0], 0)
-        deal(nc.vector.tensor_copy, w1_bf, w1_raw[1], 64)
+        deal(nc.scalar.copy, w1_bf, w1_raw[0][:], 0)
+        deal_pair(nc.vector.tensor_copy, w1_bf, w1_raw[1][:], 64, slice(0, 2))
+        deal_pair(nc.scalar.copy, w1_bf, w1_raw[1][:], 64, slice(2, 4))
         w1_op = mx_tiles("w1")
-        banks = [psum.tile([P, S], F32, name="y_ps%d" % t, tag="bank%d" % t) for t in range(PACK)]
+        halves = [slice(0, S // 2), slice(S // 2, S)]
+
+        def result_banks(name):
+            banks = [psum.tile([P, S], F32, name="%s%d" % (name, t), tag="bank%d" % t) for t in range(PACK)]
+            extra = psum.tile([P, S], F32, name=name + "_extra", tag="back0")
+            return [[banks[t][:, halves[0]], (banks[t] if t else extra)[:, halves[1]]] for t in range(PACK)], banks
+
+        y_half, banks = result_banks("y_ps")
         z = [keep.tile([P, S], F32, name="z%d" % t) for t in range(PACK)]
-        for t in range(PACK):
-            quantize(w1_op, w1_bf, slice(t * P, (t + 1) * P))
-            product(banks[t][:], w1_op, t, x_op, slice(0, S))
-            nc.scalar.copy(z[t][:], banks[t][:])
-
-        w2_bf = keep.tile([P, PACK * K], BF16, name="w2_bf", align_bytes=64)
-        w2_op = mx_tiles("w2")
-        w3_bf = keep.tile([P, PACK * K], BF16, name="w3_bf", align_bytes=64)
-        w3_op = mx_tiles("w3")
-
         z_planes = keep.tile([P, PACK, S], BF16, name="z_planes")
-        pa = [keep.tile([P, W], F32, name="pa%d" % t) for t in range(PACK)]
-        gain = [keep.tile([P, W], F32, name="gain%d" % t) for t in range(PACK)]
+        pa, gain = {}, {}
 
-        def fetch_pairs(t):
-            diff = work.tile([P, W], F32, name="diff")
+        def make_y(t):
+            quantize(w1_op, w1_bf, slice(t * P, (t + 1) * P))
+            if t == 0:
+                for h, cols in enumerate(halves):
+                    product(y_half[t][h], w1_op, t, x_op, cols)
+                    nc.scalar.copy(z[t][:, cols], y_half[t][h])
+            else:
+                product(banks[t][:], w1_op, t, x_op, slice(0, S))
+                nc.scalar.copy(z[t][:], banks[t][:])
+
+        def fetch_first(t):
+            pa[t] = keep.tile([P, W], F32, name="pa%d" % t)
             nc.vector.tensor_copy(pa[t][:], z[t][:].indirect(n1_t[:]))
+
+        def fetch_second(t):
+            diff = work.tile([P, W], F32, name="diff")
+            gain[t] = keep.tile([P, W], F32, name="gain%d" % t, align_bytes=64)
             nc.vector.tensor_tensor(diff[:], z[t][:].indirect(n2_t[:]), pa[t][:], ALU.subtract)
             nc.scalar.activation(gain[t][:], diff[:], ACT.Relu)
 
         def put_back(t):
             nc.vector.tensor_tensor(z[t][:].indirect(n1_t[:]), pa[t][:], gain[t][:], ALU.add)
-            copy = nc.vector.tensor_copy if t == PACK - 1 else nc.scalar.copy
-            copy(z_planes[:, t, :], z[t][:])
 
-        fetch_pairs(0)
-        for t in range(PACK):
-            if t + 1 < PACK:
-                fetch_pairs(t + 1)
-            put_back(t)
-            if t == 0:
-                deal(nc.scalar.copy, w2_bf, w2_raw, 0)
-            if t == 1:
-                quantize(w2_op, w2_bf, slice(0, K))
-                weave(nc.scalar.copy, w3_bf[:], w3_raw[:])
+        def round_plane(t):
+            if t < PACK - 1:
+                nc.scalar.copy(z_planes[:, t, :], z[t][:])
+            else:
+                for cols in halves:
+                    nc.vector.tensor_copy(z_planes[:, t, cols], z[t][:, cols])
 
-        z_bf = keep.tile([P, PACK * S], BF16, name="z_bf", align_bytes=64)
-        weave(nc.vector.tensor_copy, z_bf[:, : PACK * Z_SPLIT], z_planes[:, :, :Z_SPLIT])
+        def deal_w2(q):
+            deal(nc.scalar.copy, w2_bf, w2_raw[:, :, q * P : (q + 1) * P], q * P // PACK)
+
+        def weave_w3(q):
+            weave(nc.scalar.copy, w3_bf[:, q * K : (q + 1) * K], w3_raw[:, :, q * P : (q + 1) * P])
+
+        w2_bf = keep.tile([P, PACK * K], BF16, name="w2_bf", align_bytes=64)
+        w3_bf = keep.tile([P, PACK * K], BF16, name="w3_bf", align_bytes=64)
+        w2_op = mx_tiles("w2")
+        make_y(0)
+        make_y(1)
+        fetch_first(0)
+        fetch_second(0)
+        make_y(2)
+        make_y(3)
+        fetch_first(1)
+        fetch_second(1)
+        for q in range(PACK):
+            deal_w2(q)
+        quantize(w2_op, w2_bf, slice(0, K))
+        put_back(0)
+        round_plane(0)
+        fetch_first(2)
+        fetch_second(2)
+        put_back(1)
+        round_plane(1)
+        fetch_first(3)
+        fetch_second(3)
+        for q in range(PACK):
+            weave_w3(q)
+        put_back(2)
+        round_plane(2)
+        put_back(3)
+        round_plane(3)
+
+        z_bf = keep.tile([P, PACK * S], BF16, name="z_bf", tag="staging", align_bytes=64)
+        for c0, c1 in ((0, S // 2), (S // 2, Z_SPLIT)):
+            weave(nc.vector.tensor_copy, z_bf[:, PACK * c0 : PACK * c1], z_planes[:, :, c0:c1])
         weave(nc.scalar.copy, z_bf[:, PACK * Z_SPLIT :], z_planes[:, :, Z_SPLIT:])
         z_op = mx_tiles("z")
-        halves = [slice(0, S // 2), slice(S // 2, S)]
         for cols in halves:
             quantize(z_op, z_bf, cols)
+        w3_op = (
+            keep.tile([P, K], U32, name="w3_codes", tag="staging", align_bytes=64),
+            keep.tile([P, K], U8, name="w3_scales", align_bytes=64),
+        )
         quantize(w3_op, w3_bf, slice(0, K))
 
-        banks = [psum.tile([P, S], F32, name="h_ps%d" % t, tag="bank%d" % t) for t in range(PACK)]
+        h_half, banks = result_banks("h_ps")
         half_h = [keep.tile([P, S], F32, name="half_h%d" % t) for t in range(PACK)]
         here = keep.tile([P, PACK, S], F32, name="here")
         for t in range(PACK):
-            for cols in halves:
-                product(banks[t][:, cols], w2_op, t, z_op, cols)
-            nc.scalar.activation(half_h[t][:], banks[t][:], ACT.Copy, scale=0.5)
-            nc.scalar.activation(here[:, t, :], banks[t][:], ACT.Copy, scale=0.5)
+            for h, cols in enumerate(halves):
+                product(h_half[t][h], w2_op, t, z_op, cols)
+            if t == 0:
+                nc.scalar.activation(half_h[t][:, halves[0]], h_half[t][0], ACT.Copy, scale=0.5)
+                nc.vector.tensor_copy(here[:, t, halves[0]], half_h[t][:, halves[0]])
+                nc.scalar.activation(half_h[t][:, halves[1]], h_half[t][1], ACT.Copy, scale=0.5)
+            else:
+                nc.scalar.activation(half_h[t][:], banks[t][:], ACT.Copy, scale=0.5)
+                nc.scalar.copy(here[:, t, halves[0]], half_h[t][:, halves[0]])
+        for t in range(PACK):
+            nc.scalar.copy(here[:, t, halves[1]], half_h[t][:, halves[1]])
+
+        def turn_and_add(dst, terms):
+            for n, term in enumerate(terms):
+                nc.tensor.matmul(dst, term, identity[:], start=n == 0, stop=n == len(terms) - 1, is_transpose=True)
 
         z2_bf = keep.tile([P, PACK * S], BF16, name="z2_bf", align_bytes=64)
         z2_op = mx_tiles("z2")
         out_view = out.rearrange("(b p) j -> p b j", p=P)
-        for j0, width in BLOCKS:
-            cols = slice(j0, j0 + width)
-            entries = slice(j0 // 16, (j0 + width) // 16)
-            z2 = work.tile([P, PACK, width], F32, name="z2")
-            da = work.tile([P, PACK, width], F32, name="da")
-            db = work.tile([P, PACK, width], F32, name="db")
-            up = work.tile([P, PACK, width], F32, name="up")
+
+        def sum_by_turning(up, down, block):
+            cols = slice(block * P, (block + 1) * P)
+            lift = work.tile([P, PACK, P], F32, name="lift")
+            nc.scalar.activation(lift[:], down, ACT.Copy, scale=-1.0)
+            turned = psum.tile([P, PACK, P], F32, name="turned", tag="turn", bufs=2)
+            for t in range(PACK):
+                turn_and_add(turned[:, t, :], [here[:, t, cols], up[:, t, :], up[:, t, :], lift[:, t, :]])
+            rows = keep.tile([P, 2, P, 2], BF16, name="rows%d" % block)
+            nc.scalar.copy(rows[:], turned[:].rearrange("j (u e) p -> j u p e", e=2))
+            words = rows[:].rearrange("j u p e -> j (u p e)").bitcast(F32)
+            back = psum.tile([P, 2, P], F32, name="back%d" % (block % 2))
+            for u in range(2):
+                turn_and_add(back[:, u, :], [words[:, u * P : (u + 1) * P]])
+            nc.scalar.copy(
+                z2_bf[:, PACK * cols.start : PACK * cols.stop].bitcast(F32).rearrange("p (j u) -> p j u", u=2),
+                back[:].rearrange("p u j -> p j u"),
+            )
+
+        def finish(span, group, bank_no):
+            count, width = group.stop - group.start, span.stop - span.start
+            acc = psum.tile([P, count, width], F32, name="acc", tag="bank%d" % bank_no)
+            for b in range(count):
+                product(acc[:, b, :], w3_op, group.start + b, z2_op, span)
+            result = keep.tile([P, count, width], F32, name="result%d" % bank_no)
+            nc.vector.tensor_tensor(result[:], acc[:], res_t[:, group, span], ALU.add)
+            nc.sync.dma_start(out_view[:, group, span], result[:])
+            return result
+
+        def compare(span, up_tag):
+            width = span.stop - span.start
+            entries = slice(span.start // 16, span.stop // 16)
+            da = keep.tile([P, PACK, width], F32, name="da")
+            db = keep.tile([P, PACK, width], F32, name="db")
+            up = keep.tile([P, PACK, width], F32, name="up", tag=up_tag)
             down = work.tile([P, PACK, width], F32, name="down")
-            both = work.tile([P, PACK, width], F32, name="both")
-            pairs = [slice(0, 2), slice(2, 4)]
-            for pair in pairs:
-                for t in range(pair.start, pair.stop):
-                    nc.vector.tensor_tensor(da[:, t, :], half_h[t][:].indirect(n3_t[:, entries]), here[:, t, cols], ALU.subtract)
-                    nc.vector.tensor_tensor(db[:, t, :], half_h[t][:].indirect(n4_t[:, entries]), here[:, t, cols], ALU.subtract)
-            for pair in pairs:
-                nc.vector.scalar_tensor_tensor(up[:, pair], da[:, pair], 0.0, db[:, pair], ALU.max, ALU.max)
-                nc.vector.scalar_tensor_tensor(down[:, pair], da[:, pair], 0.0, db[:, pair], ALU.min, ALU.min)
-            for pair in pairs:
-                nc.vector.scalar_tensor_tensor(both[:, pair], up[:, pair], 2.0, down[:, pair], ALU.mult, ALU.subtract)
-            for pair in pairs:
-                nc.vector.tensor_tensor(z2[:, pair], both[:, pair], here[:, pair, cols], ALU.add)
-            copy = nc.vector.tensor_copy if j0 + width == S else nc.scalar.copy
-            weave(copy, z2_bf[:, PACK * j0 : PACK * (j0 + width)], z2[:])
-            quantize(z2_op, z2_bf, cols)
-            result = work.tile([P, PACK, width], F32, name="result")
-            per_bank = S // width
-            for b0 in range(0, PACK, per_bank):
-                acc = psum.tile([P, per_bank, width], F32, name="acc", tag="acc", bufs=3)
-                for b in range(per_bank):
-                    product(acc[:, b, :], w3_op, b0 + b, z2_op, cols)
-                nc.vector.tensor_tensor(
-                    result[:, b0 : b0 + per_bank, :], acc[:], res_t[:, b0 : b0 + per_bank, cols], ALU.add
-                )
-            nc.sync.dma_start(out_view[:, :, cols], result[:])
+            for t in range(PACK):
+                nc.vector.tensor_tensor(da[:, t, :], half_h[t][:].indirect(n3_t[:, entries]), here[:, t, span], ALU.subtract)
+                nc.vector.tensor_tensor(db[:, t, :], half_h[t][:].indirect(n4_t[:, entries]), here[:, t, span], ALU.subtract)
+            nc.vector.scalar_tensor_tensor(down[:], da[:], 0.0, db[:], ALU.min, ALU.min)
+            nc.vector.scalar_tensor_tensor(up[:], da[:], 0.0, db[:], ALU.max, ALU.max)
+            return up, down
+
+        first, second, third = slice(0, 2 * P), slice(2 * P, 3 * P), slice(3 * P, S)
+        up, down = compare(first, "up_first")
+        for block in range(2):
+            part = slice(block * P, (block + 1) * P)
+            sum_by_turning(up[:, :, part], down[:, :, part], block)
+        up, down = compare(second, "up_second")
+        sum_by_turning(up[:], down[:], 2)
+        up, down = compare(third, "rows1")
+        quantize(z2_op, z2_bf, first)
+        both = work.tile([P, PACK, P], F32, name="both")
+        nc.vector.scalar_tensor_tensor(both[:], up[:], 2.0, down[:], ALU.mult, ALU.subtract)
+        result_a = finish(first, slice(0, 2), 0)
+        nc.vector.tensor_tensor(
+            z2_bf[:, PACK * third.start :].rearrange("p (c i t) -> p c t i", i=4, t=PACK),
+            both[:].rearrange("p t (c i) -> p c t i", i=4),
+            here[:, :, third].rearrange("p t (c i) -> p c t i", i=4),
+            ALU.add,
+        )
+        quantize(z2_op, z2_bf, second)
+        quantize(z2_op, z2_bf, third)
+        finish(first, slice(2, PACK), 1)
+        finish(second, slice(0, PACK), 2)
+        finish(third, slice(0, PACK), 3)

from contextlib import ExitStack

import concourse.mybir as mybir
from concourse.masks import make_identity

K, T, S, W = 512, 2048, 512, 256
P, PACK = 128, 4
FLOPS = 3 * 2 * K * K * S

F32, BF16 = mybir.dt.float32, mybir.dt.bfloat16
I32, U32, U16, U8 = mybir.dt.int32, mybir.dt.uint32, mybir.dt.uint16, mybir.dt.uint8
FP8X4 = mybir.dt.float8_e4m3fn_x4
ALU = mybir.AluOpType
ACT = mybir.ActivationFunctionType

Z_SPLIT = 320


def tile_picked_deepfillrange_none_p_kernel(
    tc, x_words, x_scales, w1, w2, w3, res, offs, n1, n2, n3, n4, out
):
    nc = tc.nc
    with ExitStack() as ctx:
        keep = ctx.enter_context(tc.tile_pool(name="keep", bufs=1))
        work = ctx.enter_context(tc.tile_pool(name="work", bufs=2))
        psum = ctx.enter_context(tc.psum_pool(name="psum", bufs=1))

        def load_list(src, name):
            tile = keep.tile(list(src.shape), U16, name=name)
            nc.sync.dma_start(tile[:], src)
            return tile

        def load_rows(src, name):
            tile = keep.tile([P, PACK, src.shape[1]], F32, name=name)
            nc.sync.dma_start(tile[:], src.rearrange("(p j) c -> p j c", j=PACK))
            return tile

        def mx_tiles(name):
            codes = keep.tile([P, S], U32, name=name + "_codes", align_bytes=64)
            scales = keep.tile([P, S], U8, name=name + "_scales", align_bytes=64)
            return codes, scales

        def quantize(operand, grouped, cols):
            codes, scales = operand
            nc.vector.quantize_mx(
                out=codes[:, cols].bitcast(FP8X4),
                scales=scales[:, cols],
                in_=grouped[:, PACK * cols.start : PACK * cols.stop],
            )

        def product(acc, weights, tile_no, moving, cols):
            rows = slice(tile_no * P, (tile_no + 1) * P)
            nc.tensor.matmul_mx(
                out=acc,
                lhsT=weights[0][:, rows].bitcast(FP8X4),
                lhsT_scale=weights[1][:, rows],
                rhs=moving[0][:, cols].bitcast(FP8X4),
                rhs_scale=moving[1][:, cols],
                start=True,
                stop=True,
            )

        def deal(copy, grouped, raw, m0):
            count = raw.shape[2] // PACK
            dst = grouped[:].rearrange("p (t m j) -> p m j t", t=PACK, j=PACK)[:, m0 : m0 + count]
            copy(dst, raw.rearrange("p j (m t) -> p m j t", t=PACK))

        def deal_pair(copy, grouped, raw, m0, pair):
            count = raw.shape[2] // PACK
            dst = grouped[:].rearrange("p (t m j) -> p m j t", t=PACK, j=PACK)[:, m0 : m0 + count, :, pair]
            copy(dst, raw.rearrange("p j (m t) -> p m j t", t=PACK)[:, :, :, pair])

        def weave(copy, grouped, planes):
            copy(
                grouped.rearrange("p (c i j) -> p c j i", i=4, j=PACK),
                planes.rearrange("p j (c i) -> p c j i", i=4),
            )

        landed_scales = keep.tile([P, T // 4], I32, name="landed_scales")
        quadrants = [slice(32 * q, 32 * q + 4) for q in range(4)]
        for q, rows in enumerate(quadrants):
            nc.sync.dma_start(landed_scales[rows, :], x_scales[0, 4 * q : 4 * q + 4, :].bitcast(I32))
        offs_t = load_list(offs, "offs_t")
        table_words = keep.tile([P, T], I32, name="table_words")
        nc.sync.dma_start(table_words[:], x_words[0].rearrange("p n r -> p (n r)").bitcast(I32))
        w1_raw = [load_rows(w1[:, h * 256 : (h + 1) * 256], "w1_raw%d" % h) for h in range(2)]
        table_scales = keep.tile([P, T], U8, name="table_scales")
        nc.vector.memset(table_scales[:].bitcast(I32), 0)
        for rows in quadrants:
            nc.vector.tensor_copy(table_scales[rows, :].bitcast(I32), landed_scales[rows, :])
        n1_t = load_list(n1, "n1_t")
        n2_t = load_list(n2, "n2_t")
        w2_raw = load_rows(w2, "w2_raw")
        n3_t = load_list(n3, "n3_t")
        n4_t = load_list(n4, "n4_t")
        w3_raw = load_rows(w3, "w3_raw")
        res_t = keep.tile([P, PACK, S], F32, name="res_t")
        nc.sync.dma_start(res_t[:], res.rearrange("(b p) j -> p b j", p=P))

        identity = keep.tile([P, P], F32, name="identity")
        make_identity(nc, identity[:])

        x_op = mx_tiles("x")
        nc.vector.tensor_copy(x_op[1][:], table_scales[:].indirect(offs_t[:]))
        nc.vector.tensor_copy(x_op[0][:], table_words[:].bitcast(U32).indirect(offs_t[:]))

        w1_bf = keep.tile([P, PACK * K], BF16, name="w1_bf", align_bytes=64)
        deal(nc.scalar.copy, w1_bf, w1_raw[0][:], 0)
        deal_pair(nc.vector.tensor_copy, w1_bf, w1_raw[1][:], 64, slice(0, 2))
        deal_pair(nc.scalar.copy, w1_bf, w1_raw[1][:], 64, slice(2, 4))
        w1_op = mx_tiles("w1")
        halves = [slice(0, S // 2), slice(S // 2, S)]

        def result_banks(name):
            banks = [psum.tile([P, S], F32, name="%s%d" % (name, t), tag="bank%d" % t) for t in range(PACK)]
            extra = psum.tile([P, S], F32, name=name + "_extra", tag="back0")
            return [[banks[t][:, halves[0]], (banks[t] if t else extra)[:, halves[1]]] for t in range(PACK)], banks

        y_half, banks = result_banks("y_ps")
        z = [keep.tile([P, S], F32, name="z%d" % t) for t in range(PACK)]
        z_planes = keep.tile([P, PACK, S], BF16, name="z_planes")
        pa, gain = {}, {}

        def make_y(t):
            quantize(w1_op, w1_bf, slice(t * P, (t + 1) * P))
            if t == 0:
                for h, cols in enumerate(halves):
                    product(y_half[t][h], w1_op, t, x_op, cols)
                    nc.scalar.copy(z[t][:, cols], y_half[t][h])
            else:
                product(banks[t][:], w1_op, t, x_op, slice(0, S))
                nc.scalar.copy(z[t][:], banks[t][:])

        def fetch_first(t):
            pa[t] = keep.tile([P, W], F32, name="pa%d" % t)
            nc.vector.tensor_copy(pa[t][:], z[t][:].indirect(n1_t[:]))

        def fetch_second(t):
            diff = work.tile([P, W], F32, name="diff")
            gain[t] = keep.tile([P, W], F32, name="gain%d" % t, align_bytes=64)
            nc.vector.tensor_tensor(diff[:], z[t][:].indirect(n2_t[:]), pa[t][:], ALU.subtract)
            nc.scalar.activation(gain[t][:], diff[:], ACT.Relu)

        def put_back(t):
            nc.vector.tensor_tensor(z[t][:].indirect(n1_t[:]), pa[t][:], gain[t][:], ALU.add)

        def round_plane(t):
            if t < PACK - 1:
                nc.scalar.copy(z_planes[:, t, :], z[t][:])
            else:
                for cols in halves:
                    nc.vector.tensor_copy(z_planes[:, t, cols], z[t][:, cols])

        def deal_w2(q):
            deal(nc.scalar.copy, w2_bf, w2_raw[:, :, q * P : (q + 1) * P], q * P // PACK)

        def weave_w3(q):
            weave(nc.scalar.copy, w3_bf[:, q * K : (q + 1) * K], w3_raw[:, :, q * P : (q + 1) * P])

        w2_bf = keep.tile([P, PACK * K], BF16, name="w2_bf", align_bytes=64)
        w3_bf = keep.tile([P, PACK * K], BF16, name="w3_bf", align_bytes=64)
        w2_op = mx_tiles("w2")
        make_y(0)
        make_y(1)
        fetch_first(0)
        fetch_second(0)
        make_y(2)
        make_y(3)
        fetch_first(1)
        fetch_second(1)
        for q in range(PACK):
            deal_w2(q)
        quantize(w2_op, w2_bf, slice(0, K))
        put_back(0)
        round_plane(0)
        fetch_first(2)
        fetch_second(2)
        put_back(1)
        round_plane(1)
        fetch_first(3)
        fetch_second(3)
        for q in range(PACK):
            weave_w3(q)
        put_back(2)
        round_plane(2)
        put_back(3)
        round_plane(3)

        z_bf = keep.tile([P, PACK * S], BF16, name="z_bf", tag="staging", align_bytes=64)
        for c0, c1 in ((0, S // 2), (S // 2, Z_SPLIT)):
            weave(nc.vector.tensor_copy, z_bf[:, PACK * c0 : PACK * c1], z_planes[:, :, c0:c1])
        weave(nc.scalar.copy, z_bf[:, PACK * Z_SPLIT :], z_planes[:, :, Z_SPLIT:])
        z_op = mx_tiles("z")
        for cols in halves:
            quantize(z_op, z_bf, cols)
        w3_op = (
            keep.tile([P, K], U32, name="w3_codes", tag="staging", align_bytes=64),
            keep.tile([P, K], U8, name="w3_scales", align_bytes=64),
        )
        quantize(w3_op, w3_bf, slice(0, K))

        h_half, banks = result_banks("h_ps")
        half_h = [keep.tile([P, S], F32, name="half_h%d" % t) for t in range(PACK)]
        here = keep.tile([P, PACK, S], F32, name="here")
        for t in range(PACK):
            for h, cols in enumerate(halves):
                product(h_half[t][h], w2_op, t, z_op, cols)
            if t == 0:
                nc.scalar.activation(half_h[t][:, halves[0]], h_half[t][0], ACT.Copy, scale=0.5)
                nc.vector.tensor_copy(here[:, t, halves[0]], half_h[t][:, halves[0]])
                nc.scalar.activation(half_h[t][:, halves[1]], h_half[t][1], ACT.Copy, scale=0.5)
            else:
                nc.scalar.activation(half_h[t][:], banks[t][:], ACT.Copy, scale=0.5)
                nc.scalar.copy(here[:, t, halves[0]], half_h[t][:, halves[0]])
        for t in range(PACK):
            nc.scalar.copy(here[:, t, halves[1]], half_h[t][:, halves[1]])

        def turn_and_add(dst, terms):
            for n, term in enumerate(terms):
                nc.tensor.matmul(dst, term, identity[:], start=n == 0, stop=n == len(terms) - 1, is_transpose=True)

        z2_bf = keep.tile([P, PACK * S], BF16, name="z2_bf", align_bytes=64)
        z2_op = mx_tiles("z2")
        out_view = out.rearrange("(b p) j -> p b j", p=P)

        def sum_by_turning(up, down, block):
            cols = slice(block * P, (block + 1) * P)
            lift = work.tile([P, PACK, P], F32, name="lift")
            nc.scalar.activation(lift[:], down, ACT.Copy, scale=-1.0)
            turned = psum.tile([P, PACK, P], F32, name="turned", tag="turn", bufs=2)
            for t in range(PACK):
                turn_and_add(turned[:, t, :], [here[:, t, cols], up[:, t, :], up[:, t, :], lift[:, t, :]])
            rows = keep.tile([P, 2, P, 2], BF16, name="rows%d" % block)
            nc.scalar.copy(rows[:], turned[:].rearrange("j (u e) p -> j u p e", e=2))
            words = rows[:].rearrange("j u p e -> j (u p e)").bitcast(F32)
            back = psum.tile([P, 2, P], F32, name="back%d" % (block % 2))
            for u in range(2):
                turn_and_add(back[:, u, :], [words[:, u * P : (u + 1) * P]])
            nc.scalar.copy(
                z2_bf[:, PACK * cols.start : PACK * cols.stop].bitcast(F32).rearrange("p (j u) -> p j u", u=2),
                back[:].rearrange("p u j -> p j u"),
            )

        def finish(span, group, bank_no):
            count, width = group.stop - group.start, span.stop - span.start
            acc = psum.tile([P, count, width], F32, name="acc", tag="bank%d" % bank_no)
            for b in range(count):
                product(acc[:, b, :], w3_op, group.start + b, z2_op, span)
            result = keep.tile([P, count, width], F32, name="result%d" % bank_no)
            nc.vector.tensor_tensor(result[:], acc[:], res_t[:, group, span], ALU.add)
            nc.sync.dma_start(out_view[:, group, span], result[:])
            return result

        def compare(span, up_tag):
            width = span.stop - span.start
            entries = slice(span.start // 16, span.stop // 16)
            da = keep.tile([P, PACK, width], F32, name="da")
            db = keep.tile([P, PACK, width], F32, name="db")
            up = keep.tile([P, PACK, width], F32, name="up", tag=up_tag)
            down = work.tile([P, PACK, width], F32, name="down")
            for t in range(PACK):
                nc.vector.tensor_tensor(da[:, t, :], half_h[t][:].indirect(n3_t[:, entries]), here[:, t, span], ALU.subtract)
                nc.vector.tensor_tensor(db[:, t, :], half_h[t][:].indirect(n4_t[:, entries]), here[:, t, span], ALU.subtract)
            nc.vector.scalar_tensor_tensor(down[:], da[:], 0.0, db[:], ALU.min, ALU.min)
            nc.vector.scalar_tensor_tensor(up[:], da[:], 0.0, db[:], ALU.max, ALU.max)
            return up, down

        first, second, third = slice(0, 2 * P), slice(2 * P, 3 * P), slice(3 * P, S)
        up, down = compare(first, "up_first")
        for block in range(2):
            part = slice(block * P, (block + 1) * P)
            sum_by_turning(up[:, :, part], down[:, :, part], block)
        up, down = compare(second, "up_second")
        sum_by_turning(up[:], down[:], 2)
        up, down = compare(third, "rows1")
        quantize(z2_op, z2_bf, first)
        both = work.tile([P, PACK, P], F32, name="both")
        nc.vector.scalar_tensor_tensor(both[:], up[:], 2.0, down[:], ALU.mult, ALU.subtract)
        result_a = finish(first, slice(0, 2), 0)
        nc.vector.tensor_tensor(
            z2_bf[:, PACK * third.start :].rearrange("p (c i t) -> p c t i", i=4, t=PACK),
            both[:].rearrange("p t (c i) -> p c t i", i=4),
            here[:, :, third].rearrange("p t (c i) -> p c t i", i=4),
            ALU.add,
        )
        quantize(z2_op, z2_bf, second)
        quantize(z2_op, z2_bf, third)
        finish(first, slice(2, PACK), 1)
        finish(second, slice(0, PACK), 2)
        finish(third, slice(0, PACK), 3)
